import numpy as np, ml_dtypes
CORES = [76,84,92,100,108,116,124]
N = 7
import mx_ref
NC, G, D = 128, 4, 8
C = np.float32(0.029)
BF = ml_dtypes.bfloat16
def cut(t, i, w=512):
    return t[:, w * i:w * i + w]
def tile(rs):
    return np.stack(rs, axis=2).reshape(128, -1).astype(BF)
def layer(w, X):
    out = []
    for i in range(G):
        for t in range(len(X)):
            p = mx_ref.matmul(mx_ref.quantize(cut(w, len(X) * i + t)), X[t])
            z = p if t == 0 else z + p
        out.append(z)
    return out
def act(Z):
    return [np.maximum(z, 0) * C for z in Z]
def setup_inputs(rng):
    def f(*shape):
        return mx_ref.flush((rng.standard_normal(shape, dtype=np.float32) * np.exp2(rng.integers(-2, 3, shape[:-1] + (1,)))).astype(BF))
    return {"x": f(N, 128, 4 * NC), "w1": f(N, 128, G * 512), "wt": f(N, 128, 3 * 512)}
def setup_inputs_blocks(rng):
    d = setup_inputs(rng)
    for k in ("x", "wt", "w1"): d[k] = mx_ref.spread(d[k], rng, 2)
    return d
def setup_inputs_wide(rng):
    d = setup_inputs(rng)
    for k in ("wt",): d[k] = mx_ref.flush((d[k].astype(np.float32) * np.exp2(rng.integers(-6, 7, (N, 1, 1))).astype(np.float32)).astype(BF))
    return d
def setup_inputs_zeros(rng):
    d = setup_inputs(rng); v = d["x"].reshape(N, 128, -1, 4).copy()
    v[np.broadcast_to((rng.random((N, 1, v.shape[2], 1)) < 0.33), v.shape)] = 0
    d["x"] = v.reshape(d["x"].shape)
    return d
def reference(x, w1, wt):
    h = [tile(act(layer(w1[j], [mx_ref.quantize(x[j])]))) for j in range(N)]
    y = np.zeros((N, 128, NC), np.float32)
    for r in range(N):
        e = np.concatenate([h[(r - 1) % N][:, 4 * (NC - D):], h[r], h[(r + 1) % N][:, :4 * D]], axis=1)
        for t in range(3):
            p = mx_ref.matmul(mx_ref.quantize(cut(wt[r], t)), mx_ref.quantize(e[:, 4 * D * t:4 * D * t + 4 * NC]))
            y[r] = p if t == 0 else y[r] + p
    return {"y": y}

import numpy as np
from concourse.bass import DstId, RemoteDMATransfer
from concourse.mybir import dt, AluOpType, ActivationFunctionType

OWN = 32
EDGE = 32
NC, D = 128, 8
C = float(np.float32(0.029))
SPLIT = 3

SCRATCH = {
    "xt": ("sbuf", [128, 512], "bfloat16"),
    "w1t": ("sbuf", [128, 2048], "bfloat16"),
    "wtt": ("sbuf", [128, 1536], "bfloat16"),
    "h": ("sbuf", [128, 512], "bfloat16"),
    "he": ("sbuf", [128, 512], "bfloat16"),
    "xc": ("sbuf", [128, 256], "float8_e4m3fn_x4"),
    "xs": ("sbuf", [128, 256], "uint8"),
    "w1c": ("sbuf", [128, 512], "float8_e4m3fn_x4"),
    "w1s": ("sbuf", [128, 512], "uint8"),
    "wtc": ("sbuf", [128, 384], "float8_e4m3fn_x4"),
    "wts": ("sbuf", [128, 384], "uint8"),
    "hec": ("sbuf", [128, 128], "float8_e4m3fn_x4"),
    "hes": ("sbuf", [128, 128], "uint8"),
    "ec": ("sbuf", [128, 192], "float8_e4m3fn_x4"),
    "es": ("sbuf", [128, 192], "uint8"),
    "rc": ("sbuf", [128, 16], "float8_e4m3fn_x4"),
    "rs": ("sbuf", [128, 64], "uint8"),
    "yt": ("sbuf", [128, 128], "float32"),
    "z": ("psum", [128, 2048], "float32"),
    "yp": ("psum", [128, 512], "float32"),
}
SEMAPHORES = ["ldx", "ldwa", "ldwb", "ldwt", "fill", "qx", "qa0", "qa1", "qa2", "qa3", "mm0", "mm1", "mm2", "mm3",
              "edges", "edge3", "qe", "hs", "hv", "qh", "qw", "taps", "ycopy", "stored",
              "relay", "left", "right", "sent"]


def engines(mask):
    return [1 << e for e in range(mask.bit_length()) if mask >> e & 1]


def plan(T, topo, rank):
    me = T.cores[rank]
    n = len(T.cores)
    out = []
    for off, to, side in ((0, (rank + 1) % n, "left"), (D, (rank - 1) % n, "right")):
        dst = T.cores[to]
        a, b = topo.chip(me), topo.chip(dst)
        hops = 0 if topo.may_write(me, dst) else 1 if topo.mates(a, b) else 2
        out.append((off, dst, side, hops))
    return out


def relays(T, topo, rank):
    me = T.cores[rank]
    far = [dst for _, dst, _, hops in plan(T, topo, rank) if hops]
    c0 = me
    while c0 > 0 and topo.chip(c0 - 1) == topo.chip(me):
        c0 -= 1
    cand = []
    c = c0
    while len(cand) < 64 and c < c0 + 64:
        if c < 128 and topo.chip(c) == topo.chip(me) and c != me and T.rank_of(c) is None:
            if all(topo.may_write(c, d) for d in far):
                cand.append(c)
        c += 1
    cand.sort(key=lambda k: (topo.die(k) != topo.die(me), k))
    return cand[0], cand[1]


def dst_id(topo, core):
    rid, pid, _ = topo.addr(core)
    return DstId(rid=rid, pnc=pid)


HALF = 4


def halo(T, side):
    a = OWN - D if side == "left" else OWN + NC
    return a, a + D


def relay_program(g, core, T, topo, rank, scales):
    p = plan(T, topo, rank)
    far = sorted([e for e in p if e[3]], key=lambda e: -e[3])
    g.wait_ge(T.sem.relay, HALF)
    n = 0
    for off, dst, side, _ in far:
        rid, pid, _ = topo.addr(dst)
        m = topo.mask(core, dst)
        a, b = halo(T, side)
        if scales:
            g.remote_dma(T.es[:, a:b], T.rs[:, off:off + D], T.sem[side], T.sem.sent, pid, rid, m)
        else:
            g.remote_dma(T.ec[:, a:b].bitcast(dt.uint8), T.rc[:, off:off + D].bitcast(dt.uint8),
                         T.sem[side], T.sem.sent, pid, rid, m)
        n += len(engines(m))
    g.wait_ge(T.sem.sent, n)


def rank_program(g, core, T, topo):
    rank = T.rank_of(core)
    if rank is None:
        for r in range(len(T.cores)):
            if topo.chip(core) == topo.chip(T.cores[r]):
                two = relays(T, topo, r)
                if core in two:
                    relay_program(g, core, T, topo, r, core == two[1])
        return
    s = T.sem
    relu = ActivationFunctionType.Relu

    cut = 512 * SPLIT
    g.sync.dma_start(T.xt[:], T.x[:]).then_inc(s.ldx, 16)
    g.scalar.dma_start(T.w1t[:, 0:cut], T.w1[:, 0:cut]).then_inc(s.ldwa, 16)
    g.sync.dma_start(T.w1t[:, cut:2048], T.w1[:, cut:2048]).then_inc(s.ldwb, 16)
    g.sync.dma_start(T.wtt[:], T.wt[:]).then_inc(s.ldwt, 16)

    v = g.vector
    v.memset(T.he[:], 0.0).then_inc(s.fill, 1)
    v.wait_ge(s.ldx, 16)
    v.quantize_mx(T.xc[:, 0:128], T.xs[:, 0:128], T.xt[:]).then_inc(s.qx, 1)
    v.quantize_mx(T.xc[:, 128:256], T.xs[:, 128:256], T.xt[:]).then_inc(s.qx, 1)
    for i in range(4):
        if i == 0:
            v.wait_ge(s.ldwa, 16)
        if i == SPLIT:
            v.wait_ge(s.ldwb, 16)
        v.quantize_mx(T.w1c[:, 128 * i:128 * i + 128], T.w1s[:, 128 * i:128 * i + 128],
                      T.w1t[:, 512 * i:512 * i + 512]).then_inc(s["qa%d" % i], 1)

    t = g.tensor
    t.wait_ge(s.qx, 2)
    for i in range(4):
        t.wait_ge(s["qa%d" % i], 1)
        t.matmul_mx(T.z[:, 512 * i:512 * i + 128], T.w1c[:, 128 * i:128 * i + 128], T.w1s[:, 128 * i:128 * i + 128],
                    T.xc[:, 64:192], T.xs[:, 64:192], True, True).then_inc(s["mm%d" % i], 1)

    e0 = NC // 2 - D
    q = g.scalar
    q.wait_ge(s.fill, 1)
    for i in range(3):
        q.wait_ge(s["mm%d" % i], 1)
        q.activation(T.he[:, 4 * EDGE + i:4 * EDGE + 8 * D:4], T.z[:, 512 * i + e0:512 * i + e0 + 2 * D],
                     relu, scale=C).then_inc(s.edges, 1)
    for i in range(3):
        q.activation(T.h[:, 256 + i:512:4], T.z[:, 512 * i:512 * i + 64], relu, scale=C).then_inc(s.hs, 1)
        q.activation(T.h[:, i:256:4], T.z[:, 512 * i + 64:512 * i + 128], relu, scale=C).then_inc(s.hs, 1)

    v.wait_ge(s.fill, 1)
    v.wait_ge(s.mm3, 1)
    v.tensor_scalar(T.he[:, 4 * EDGE + 3:4 * EDGE + 8 * D:4], T.z[:, 1536 + e0:1536 + e0 + 2 * D], 0.0, C,
                    AluOpType.max, AluOpType.mult).then_inc(s.edge3, 1)
    v.wait_ge(s.edges, 3)
    v.wait_ge(s.edge3, 1)
    v.quantize_mx(T.hec[:], T.hes[:], T.he[:]).then_inc(s.qe, 1)
    v.tensor_scalar(T.h[:, 259:512:4], T.z[:, 1536:1600], 0.0, C, AluOpType.max, AluOpType.mult).then_inc(s.hv, 1)
    v.tensor_scalar(T.h[:, 3:256:4], T.z[:, 1600:1664], 0.0, C, AluOpType.max, AluOpType.mult).then_inc(s.hv, 1)
    v.wait_ge(s.hs, 6)
    v.wait_ge(s.hv, 2)
    v.quantize_mx(T.ec[:, OWN:OWN + NC], T.es[:, OWN:OWN + NC], T.h[:]).then_inc(s.qh, 1)
    v.wait_ge(s.ldwt, 16)
    v.quantize_mx(T.wtc[:], T.wts[:], T.wtt[:]).then_inc(s.qw, 1)

    p = plan(T, topo, rank)
    far = [e for e in p if e[3]]
    near = [e for e in p if not e[3]]
    sent = 0
    g.wait_ge(s.qe, 1)
    if far:
        rel = relays(T, topo, rank)
        lo = min(e[0] for e in far)
        w = D * len(far)
        en = engines(topo.mask(core, rel[0]) & topo.mask(core, rel[1]))
        g.remote_dma_fused([
            RemoteDMATransfer(dst_ids=[dst_id(topo, rel[0])], dma_engine_mask=sum(en[:HALF]), remote_sem=s.relay,
                              src=T.hec[:, EDGE + lo:EDGE + lo + w].bitcast(dt.uint8),
                              dst=T.rc[:, lo:lo + w].bitcast(dt.uint8)),
            RemoteDMATransfer(dst_ids=[dst_id(topo, rel[1])], dma_engine_mask=sum(en[HALF:2 * HALF]), remote_sem=s.relay,
                              src=T.hes[:, EDGE + lo:EDGE + lo + 4 * w],
                              dst=T.rs[:, lo:lo + 4 * w]),
        ], local_sem=s.sent)
        sent += 2 * HALF
    for off, dst, side, _ in near:
        a, b = halo(T, side)
        en = engines(topo.mask(core, dst))
        if side == "left":
            sa, da = EDGE + off + D - 4 * D, b - 4 * D
        else:
            sa, da = EDGE + off, a
        g.remote_dma_fused([
            RemoteDMATransfer(dst_ids=[dst_id(topo, dst)], dma_engine_mask=sum(en[:HALF]), remote_sem=s[side],
                              src=T.hec[:, EDGE + off:EDGE + off + D].bitcast(dt.uint8),
                              dst=T.ec[:, a:b].bitcast(dt.uint8)),
            RemoteDMATransfer(dst_ids=[dst_id(topo, dst)], dma_engine_mask=sum(en[HALF:2 * HALF]), remote_sem=s[side],
                              src=T.hes[:, sa:sa + 4 * D], dst=T.es[:, da:da + 4 * D]),
        ], local_sem=s.sent)
        sent += 2 * HALF
    g.wait_ge(s.sent, sent)

    n = len(T.cores)
    halos = []
    for src, side, tap in (((rank - 1) % n, "left", 0), ((rank + 1) % n, "right", 2)):
        for _, dst, sd, hops in plan(T, topo, src):
            if dst == core and sd == side:
                two = relays(T, topo, src) if hops else None
                cnt = 2 * len(engines(topo.mask(two[0], core))) if hops else 2 * HALF
                halos.append((hops, side, tap, cnt))
    halos.sort()

    def tap_mm(k, start, stop):
        return t.matmul_mx(T.yp[:, 0:NC], T.wtc[:, 128 * k:128 * k + 128], T.wts[:, 128 * k:128 * k + 128],
                           T.ec[:, OWN - D + D * k:OWN - D + D * k + NC], T.es[:, OWN - D + D * k:OWN - D + D * k + NC],
                           start, stop)

    t.wait_ge(s.qh, 1)
    t.wait_ge(s.qw, 1)
    tap_mm(1, True, False)
    t.wait_ge(s[halos[0][1]], halos[0][3])
    tap_mm(halos[0][2], False, False)
    t.wait_ge(s[halos[1][1]], halos[1][3])
    tap_mm(halos[1][2], False, True).then_inc(s.taps, 1)

    v.wait_ge(s.taps, 1)
    v.tensor_copy(T.yt[:], T.yp[:, 0:NC]).then_inc(s.ycopy, 1)
    g.sync.wait_ge(s.ycopy, 1)
    g.sync.dma_start(T.y[:], T.yt[:]).then_inc(s.stored, 16)
    g.sync.wait_ge(s.stored, 16)
